import numpy as np
import ml_dtypes


def mxq(x, axis, fmt="e4m3"):
    dtype, down = {"e4m3": (ml_dtypes.float8_e4m3fn, 7), "e5m2": (ml_dtypes.float8_e5m2, 14)}[fmt]
    v = np.moveaxis(np.asarray(x, np.float32).astype(ml_dtypes.bfloat16).astype(np.float64), axis, -1)
    blocks = v.reshape(v.shape[:-1] + (-1, 32))
    amax = np.abs(blocks).max(-1, keepdims=True)
    byte = np.maximum(np.where(amax > 0, np.frexp(amax)[1] - 1 + 127, 0) - down, 1)
    scale = np.exp2(byte - 127.0)
    codes = (blocks / scale).astype(np.float32).astype(dtype).astype(np.float64)
    return np.moveaxis((codes * scale).reshape(v.shape), -1, axis)


WIDE = False


def mx_kscale(k):
    if not WIDE:
        return np.ones(k)
    levels = np.array([10, -10, 5, -5, 0])
    if k % 512:
        return np.exp2(np.random.permutation(np.resize(levels, k // 32))).repeat(32)
    a = np.empty((k // 512, 16))
    for p in range(k // 512):
        a[p, :8] = np.random.permutation(np.resize(levels, 8))
        for g in range(8):
            far = levels[np.abs(levels - a[p, g]) >= 10]
            a[p, g + 8] = far[np.random.randint(len(far))]
    return np.exp2(a.ravel()).repeat(32)


def f64(x):
    return np.asarray(x).astype(np.float64)


def striped(idx):
    return np.tile(idx.reshape(-1, 16).T, (8, 1)).astype(np.uint16)


def unstriped(offs):
    return offs[:16].T.reshape(-1).astype(np.int64)


def pack_weight(w):
    k, n = w.shape
    w = f64(np.asarray(w, np.float32).astype(ml_dtypes.bfloat16)).reshape(k // 32, 32, n)
    amax = np.abs(w).max(1)
    byte = np.clip(np.where(amax > 0, np.frexp(amax)[1] - 1 + 127 - 7, 1), 1, 254)
    scaled = (w * np.exp2(127.0 - byte)[:, None, :]).reshape(k, n).astype(np.float32)
    words = np.ascontiguousarray(scaled.reshape(k // 512, 128, 4, n).transpose(0, 1, 3, 2)).astype(ml_dtypes.float8_e4m3fn).view(np.uint8)
    return words, np.ascontiguousarray(byte.astype(np.uint8).reshape(k // 512, 16, n))


def unpack_weight(words, scales):
    g, p, n, _ = words.shape
    vals = np.ascontiguousarray(words).view(ml_dtypes.float8_e4m3fn).astype(np.float64) * np.repeat(np.exp2(scales.astype(np.float64) - 127.0), 8, axis=1)[..., None]
    return vals.transpose(0, 1, 3, 2).reshape(g * 512, n)


K, T, S, D, N = 1024, 2048, 1024, 4, 128


def setup_inputs():
    n = np.random.standard_normal
    s = mx_kscale(K)[:, None]
    packed_xT = pack_weight(n((K, T)) * s)
    return {
        "x_words": packed_xT[0],
        "x_scales": packed_xT[1],
        "w1": (n((K, N)) / np.sqrt(K) / s).astype(np.float32),
        "w2": (n((K, N)) / np.sqrt(K) / s).astype(np.float32),
        "ca": (-0.5 * n((N, 1))).astype(np.float32),
        "thb": (-0.5 * n((N, 1))).astype(np.float32),
        "offs": striped(np.random.permutation(T)[:S]),
    }


def reference(x_words, x_scales, w1, w2, ca, thb, offs):
    xq = unpack_weight(x_words, x_scales)[:, unstriped(offs)]
    a0 = (mxq(f64(w1), 0, "e4m3").T @ xq) + f64(ca)
    b0 = (mxq(f64(w2), 0, "e4m3").T @ xq) + f64(thb)
    b6 = b0 + 6.0
    e1 = np.maximum(b6, np.pad(b6, ((0, 0), (0, 1)))[:, 1:])
    imp = np.maximum(-1.0 * a0, np.maximum(e1, np.pad(e1, ((0, 0), (0, 2)))[:, 2:]) - 6.0)
    return imp.reshape(len(imp), -1, D).min(axis=2)

@@ -1,0 +1,207 @@
+from contextlib import ExitStack
+
+import concourse.mybir as mybir
+
+K, T, S, D, N = 1024, 2048, 1024, 4, 128
+FLOPS = 2 * K * (2 * N) * S
+
+F32 = mybir.dt.float32
+BF16 = mybir.dt.bfloat16
+I32 = mybir.dt.int32
+U32 = mybir.dt.uint32
+U16 = mybir.dt.uint16
+U8 = mybir.dt.uint8
+FP8X4 = mybir.dt.float8_e4m3fn_x4
+ALU = mybir.AluOpType
+ACT = mybir.ActivationFunctionType
+
+P = 128
+PACK = 4
+K_PASS = P * PACK
+PASSES = K // K_PASS
+HALF = 512
+GROUPS = HALF // D
+PITCH = GROUPS + 4
+PAD = -6.0
+
+
+def tile_picked_ystl_hard_p_kernel(tc, x_words, x_scales, w1, w2, ca, thb, offs, out):
+    nc = tc.nc
+    with ExitStack() as ctx:
+        keep = ctx.enter_context(tc.tile_pool(name="keep", bufs=1))
+        psum = ctx.enter_context(tc.psum_pool(name="psum", bufs=1))
+
+        offsets = keep.tile([P, S // 16], U16, name="offsets")
+        nc.sync.dma_start(offsets[:], offs)
+
+        table_scales = keep.tile([P, T], U8, name="table_scales", align_bytes=64)
+        nc.vector.memset(table_scales[:].bitcast(I32), 0)
+        for q in range(4):
+            nc.sync.dma_start(
+                table_scales[32 * q : 32 * q + 8, :].bitcast(I32),
+                x_scales[:, 4 * q : 4 * q + 4, :].bitcast(I32),
+            )
+
+        table_words = [keep.tile([P, T], I32, name=f"table_words{o}", align_bytes=64) for o in range(PASSES)]
+        raw = {}
+
+        def load_words(o):
+            nc.sync.dma_start(table_words[o][:], x_words[o].rearrange("p n t -> p (n t)").bitcast(I32))
+
+        def load_weight(key, w, o):
+            raw[key, o] = keep.tile([P, PACK, N], F32, name=f"raw_{key}{o}", align_bytes=64)
+            nc.sync.dma_start(raw[key, o][:], w[o * K_PASS : (o + 1) * K_PASS, :].rearrange("(p j) m -> p j m", j=PACK))
+
+        thb_col = keep.tile([P, 1], F32, name="thb_col")
+        ca_col = keep.tile([P, 1], F32, name="ca_col")
+
+        load_words(0)
+        nc.sync.dma_start(thb_col[:], thb)
+        nc.sync.dma_start(ca_col[:], ca)
+        load_weight("b", w2, 0)
+        load_weight("a", w1, 0)
+        load_words(1)
+        load_weight("b", w2, 1)
+        load_weight("a", w1, 1)
+
+        minus_ca = keep.tile([P, 1], F32, name="minus_ca")
+        nc.scalar.activation(minus_ca[:], ca_col[:], ACT.Copy, scale=-1.0)
+
+        codes, scales = {}, {}
+
+        def cast(key, o, sign):
+            grouped = keep.tile([P, N, PACK], BF16, name=f"grouped_{key}{o}", tag=f"slot_{key}{o}", align_bytes=64)
+            nc.scalar.activation(grouped[:], raw[key, o][:].rearrange("p j m -> p m j"), ACT.Copy, scale=sign)
+            return grouped
+
+        def quantise(key, o, grouped):
+            codes[key, o] = keep.tile([P, N], U32, name=f"codes_{key}{o}", align_bytes=64)
+            scales[key, o] = keep.tile([P, N], U8, name=f"scales_{key}{o}", align_bytes=64)
+            nc.vector.quantize_mx(
+                out=codes[key, o][:].bitcast(FP8X4),
+                scales=scales[key, o][:],
+                in_=grouped[:].rearrange("p m j -> p (m j)"),
+            )
+
+        picked, picked_scales = {}, {}
+
+        def gather_scales(h, tag):
+            picked_scales[h] = keep.tile([P, HALF], U8, name=f"picked_scales{h}", tag=tag, align_bytes=64)
+            cols = slice(h * HALF // 16, (h + 1) * HALF // 16)
+            nc.vector.tensor_copy(picked_scales[h][:], table_scales[:].indirect(offsets[:, cols]))
+
+        def gather(o, h, tag):
+            picked[o, h] = keep.tile([P, HALF], U32, name=f"picked{o}{h}", tag=tag, align_bytes=64)
+            cols = slice(h * HALF // 16, (h + 1) * HALF // 16)
+            nc.vector.tensor_copy(picked[o, h][:], table_words[o][:].bitcast(U32).indirect(offsets[:, cols]))
+
+        acc = {(key, h): psum.tile([P, HALF], F32, name=f"acc_{key}{h}") for key in ("a", "b") for h in range(2)}
+
+        def multiply(key, o, h):
+            nc.tensor.matmul_mx(
+                out=acc[key, h][:],
+                lhsT=codes[key, o][:].bitcast(FP8X4),
+                lhsT_scale=scales[key, o][:],
+                rhs=picked[o, h][:].bitcast(FP8X4),
+                rhs_scale=picked_scales[h][4 * o : P, :],
+                start=(o == 0),
+                stop=(o == PASSES - 1),
+            )
+
+        b0 = [keep.tile([P, D * PITCH], F32, name=f"b0_{h}", align_bytes=64) for h in range(2)]
+        planes = [t[:].rearrange("p (d s) -> p d s", d=D) for t in b0]
+        nc.vector.memset(planes[1][:, 0:3, GROUPS : GROUPS + 1], PAD)
+
+        def evacuate(h):
+            nc.scalar.activation(
+                planes[h][:, :, 0:GROUPS], acc["b", h][:].rearrange("p (v d) -> p d v", d=D), ACT.Identity, bias=thb_col[:]
+            )
+            if h == 1:
+                nc.scalar.activation(
+                    planes[0][:, 0:3, GROUPS : GROUPS + 1],
+                    acc["b", h][:, 0:3].rearrange("p (d v) -> p d v", v=1),
+                    ACT.Identity,
+                    bias=thb_col[:],
+                )
+
+        work = {
+            (name, h): keep.tile([P, 2, GROUPS], F32, name=f"{name}{h}", align_bytes=64)
+            for name in ("shared", "even", "odd", "low", "side")
+            for h in range(2)
+        }
+        both = [keep.tile([P, GROUPS], F32, name=f"both{h}", align_bytes=64) for h in range(2)]
+        result = [keep.tile([P, GROUPS], F32, name=f"result{h}", align_bytes=64) for h in range(2)]
+
+        def shared(h):
+            span = 2 * (PITCH - 1)
+            nc.vector.tensor_tensor(
+                work["shared", h][:],
+                b0[h][:, 1 : 1 + span].rearrange("p (c s) -> p c s", c=2)[:, :, 0:GROUPS],
+                b0[h][:, PITCH + 1 : PITCH + 1 + span].rearrange("p (c s) -> p c s", c=2)[:, :, 0:GROUPS],
+                ALU.max,
+            )
+
+        def own(h, name, d):
+            minus_a = acc["a", h][:].rearrange("p (v e d) -> p d e v", e=2, d=2)
+            nc.vector.scalar_tensor_tensor(
+                work[name, h][:], minus_a[:, d], minus_ca[:], planes[h][:, 0::2, d : GROUPS + d], ALU.add, ALU.max
+            )
+
+        def low(h, v):
+            nc.vector.tensor_tensor(work["low", h][:, :, v], work["even", h][:, :, v], work["odd", h][:, :, v], ALU.min)
+
+        def side(h, v):
+            nc.vector.tensor_tensor(work["side", h][:, :, v], work["shared", h][:, :, v], work["low", h][:, ::-1, v], ALU.max)
+
+        def meet(h, v):
+            nc.vector.tensor_tensor(both[h][:, v], work["side", h][:, 0, v], work["side", h][:, 1, v], ALU.min)
+
+        def last(h, v):
+            nc.vector.tensor_tensor(result[h][:, v], both[h][:, v], planes[h][:, 3, v], ALU.max)
+
+        def store(h):
+            nc.sync.dma_start(out[:, h * GROUPS : (h + 1) * GROUPS], result[h][:])
+
+        grouped = {}
+        for o in range(PASSES):
+            grouped["b", o] = cast("b", o, 1.0)
+            grouped["a", o] = cast("a", o, -1.0)
+
+        gather(0, 1, "picked01")
+        gather(0, 0, "picked00")
+        gather_scales(1, "picked_scales1")
+        quantise("b", 0, grouped["b", 0])
+        quantise("a", 0, grouped["a", 0])
+        multiply("b", 0, 1)
+        multiply("a", 0, 1)
+        gather_scales(0, "slot_a0")
+        multiply("b", 0, 0)
+        multiply("a", 0, 0)
+        gather(1, 1, "picked11")
+        quantise("b", 1, grouped["b", 1])
+        quantise("a", 1, grouped["a", 1])
+        multiply("b", 1, 1)
+        multiply("a", 1, 1)
+        evacuate(1)
+        gather(1, 0, "slot_a1")
+        multiply("b", 1, 0)
+        multiply("a", 1, 0)
+        evacuate(0)
+
+        whole = slice(0, GROUPS)
+        parts = (slice(0, GROUPS // 2), slice(GROUPS // 2, GROUPS))
+        own(1, "even", 0)
+        own(1, "odd", 1)
+        shared(1)
+        low(1, whole)
+        side(1, whole)
+        own(0, "even", 0)
+        meet(1, whole)
+        own(0, "odd", 1)
+        last(1, whole)
+        store(1)
+        shared(0)
+        for step in (low, side, meet, last):
+            for v in parts:
+                step(0, v)
+        store(0)

@@ -32,55 +32,54 @@ def tile_picked_ystl_hard_p_kernel(tc, x_words, x_scales, w1, w2, ca, thb, offs,
         psum = ctx.enter_context(tc.psum_pool(name="psum", bufs=1))
 
         offsets = keep.tile([P, S // 16], U16, name="offsets")
-        nc.sync.dma_start(offsets[:], offs)
-
         table_scales = keep.tile([P, T], U8, name="table_scales", align_bytes=64)
-        nc.vector.memset(table_scales[:].bitcast(I32), 0)
-        for q in range(4):
-            nc.sync.dma_start(
-                table_scales[32 * q : 32 * q + 8, :].bitcast(I32),
-                x_scales[:, 4 * q : 4 * q + 4, :].bitcast(I32),
-            )
-
         table_words = [keep.tile([P, T], I32, name=f"table_words{o}", align_bytes=64) for o in range(PASSES)]
+        thb_col = keep.tile([P, 1], F32, name="thb_col")
+        ca_col = keep.tile([P, 1], F32, name="ca_col")
         raw = {}
+
+        def load_scales():
+            for q in range(4):
+                nc.sync.dma_start(
+                    table_scales[32 * q : 32 * q + 8, :].bitcast(I32),
+                    x_scales[:, 4 * q : 4 * q + 4, :].bitcast(I32),
+                )
 
         def load_words(o):
             nc.sync.dma_start(table_words[o][:], x_words[o].rearrange("p n t -> p (n t)").bitcast(I32))
 
         def load_weight(key, w, o):
-            raw[key, o] = keep.tile([P, PACK, N], F32, name=f"raw_{key}{o}", align_bytes=64)
+            raw[key, o] = keep.tile([P, PACK, N], F32, name=f"raw_{key}{o}", tag=f"slot_{key}{o}", align_bytes=64)
             nc.sync.dma_start(raw[key, o][:], w[o * K_PASS : (o + 1) * K_PASS, :].rearrange("(p j) m -> p j m", j=PACK))
 
-        thb_col = keep.tile([P, 1], F32, name="thb_col")
-        ca_col = keep.tile([P, 1], F32, name="ca_col")
-
+        nc.vector.memset(table_scales[:].bitcast(I32), 0)
+        nc.sync.dma_start(offsets[:], offs)
         load_words(0)
-        nc.sync.dma_start(thb_col[:], thb)
-        nc.sync.dma_start(ca_col[:], ca)
         load_weight("b", w2, 0)
         load_weight("a", w1, 0)
-        load_words(1)
+        load_scales()
         load_weight("b", w2, 1)
+        load_words(1)
         load_weight("a", w1, 1)
+        nc.sync.dma_start(thb_col[:], thb)
+        nc.sync.dma_start(ca_col[:], ca)
 
-        minus_ca = keep.tile([P, 1], F32, name="minus_ca")
-        nc.scalar.activation(minus_ca[:], ca_col[:], ACT.Copy, scale=-1.0)
+        order = (("b", 0), ("a", 0), ("b", 1), ("a", 1))
+        spans = ((0, 2), (2, 3), (3, 4))
+        grouped = [keep.tile([P, hi - lo, N, PACK], BF16, name=f"grouped{lo}", align_bytes=64) for lo, hi in spans]
+        codes = [keep.tile([P, (hi - lo) * N], U32, name=f"codes{lo}", align_bytes=64) for lo, hi in spans]
+        scales = [keep.tile([P, (hi - lo) * N], U8, name=f"scales{lo}", align_bytes=64) for lo, hi in spans]
+        where = {order[i]: (s, i - lo) for s, (lo, hi) in enumerate(spans) for i in range(lo, hi)}
 
-        codes, scales = {}, {}
+        for key, o in order:
+            s, i = where[key, o]
+            nc.scalar.activation(
+                grouped[s][:, i], raw[key, o][:].rearrange("p j m -> p m j"), ACT.Copy, scale=(1.0 if key == "b" else -1.0)
+            )
 
-        def cast(key, o, sign):
-            grouped = keep.tile([P, N, PACK], BF16, name=f"grouped_{key}{o}", tag=f"slot_{key}{o}", align_bytes=64)
-            nc.scalar.activation(grouped[:], raw[key, o][:].rearrange("p j m -> p m j"), ACT.Copy, scale=sign)
-            return grouped
-
-        def quantise(key, o, grouped):
-            codes[key, o] = keep.tile([P, N], U32, name=f"codes_{key}{o}", align_bytes=64)
-            scales[key, o] = keep.tile([P, N], U8, name=f"scales_{key}{o}", align_bytes=64)
+        def quantise(s):
             nc.vector.quantize_mx(
-                out=codes[key, o][:].bitcast(FP8X4),
-                scales=scales[key, o][:],
-                in_=grouped[:].rearrange("p m j -> p (m j)"),
+                out=codes[s][:].bitcast(FP8X4), scales=scales[s][:], in_=grouped[s][:].rearrange("p i m j -> p (i m j)")
             )
 
         picked, picked_scales = {}, {}
@@ -90,19 +89,27 @@ def tile_picked_ystl_hard_p_kernel(tc, x_words, x_scales, w1, w2, ca, thb, offs,
             cols = slice(h * HALF // 16, (h + 1) * HALF // 16)
             nc.vector.tensor_copy(picked_scales[h][:], table_scales[:].indirect(offsets[:, cols]))
 
-        def gather(o, h, tag):
-            picked[o, h] = keep.tile([P, HALF], U32, name=f"picked{o}{h}", tag=tag, align_bytes=64)
+        def gather_first():
+            whole = keep.tile([P, S], U32, name="picked0", align_bytes=64)
+            nc.vector.tensor_copy(whole[:], table_words[0][:].bitcast(U32).indirect(offsets[:]))
+            for h in range(2):
+                picked[0, h] = whole[:, h * HALF : (h + 1) * HALF]
+
+        def gather_second(h, tag):
+            part = keep.tile([P, HALF], U32, name=f"picked1{h}", tag=tag, align_bytes=64)
             cols = slice(h * HALF // 16, (h + 1) * HALF // 16)
-            nc.vector.tensor_copy(picked[o, h][:], table_words[o][:].bitcast(U32).indirect(offsets[:, cols]))
+            nc.vector.tensor_copy(part[:], table_words[1][:].bitcast(U32).indirect(offsets[:, cols]))
+            picked[1, h] = part[:]
 
         acc = {(key, h): psum.tile([P, HALF], F32, name=f"acc_{key}{h}") for key in ("a", "b") for h in range(2)}
 
         def multiply(key, o, h):
+            s, i = where[key, o]
             nc.tensor.matmul_mx(
                 out=acc[key, h][:],
-                lhsT=codes[key, o][:].bitcast(FP8X4),
-                lhsT_scale=scales[key, o][:],
-                rhs=picked[o, h][:].bitcast(FP8X4),
+                lhsT=codes[s][:, i * N : (i + 1) * N].bitcast(FP8X4),
+                lhsT_scale=scales[s][:, i * N : (i + 1) * N],
+                rhs=picked[o, h].bitcast(FP8X4),
                 rhs_scale=picked_scales[h][4 * o : P, :],
                 start=(o == 0),
                 stop=(o == PASSES - 1),
@@ -126,82 +133,52 @@ def tile_picked_ystl_hard_p_kernel(tc, x_words, x_scales, w1, w2, ca, thb, offs,
 
         work = {
             (name, h): keep.tile([P, 2, GROUPS], F32, name=f"{name}{h}", align_bytes=64)
-            for name in ("shared", "even", "odd", "low", "side")
+            for name in ("pair", "shared", "even", "odd", "low", "side")
             for h in range(2)
         }
-        both = [keep.tile([P, GROUPS], F32, name=f"both{h}", align_bytes=64) for h in range(2)]
         result = [keep.tile([P, GROUPS], F32, name=f"result{h}", align_bytes=64) for h in range(2)]
 
-        def shared(h):
+        def first_stage(h):
             span = 2 * (PITCH - 1)
             nc.vector.tensor_tensor(
-                work["shared", h][:],
+                work["pair", h][:],
                 b0[h][:, 1 : 1 + span].rearrange("p (c s) -> p c s", c=2)[:, :, 0:GROUPS],
                 b0[h][:, PITCH + 1 : PITCH + 1 + span].rearrange("p (c s) -> p c s", c=2)[:, :, 0:GROUPS],
                 ALU.max,
             )
-
-        def own(h, name, d):
             minus_a = acc["a", h][:].rearrange("p (v e d) -> p d e v", e=2, d=2)
-            nc.vector.scalar_tensor_tensor(
-                work[name, h][:], minus_a[:, d], minus_ca[:], planes[h][:, 0::2, d : GROUPS + d], ALU.add, ALU.max
+            for d, name in enumerate(("even", "odd")):
+                nc.vector.scalar_tensor_tensor(
+                    work[name, h][:], minus_a[:, d], ca_col[:], planes[h][:, 0::2, d : GROUPS + d], ALU.subtract, ALU.max
+                )
+            nc.vector.tensor_tensor(
+                work["shared", h][:], work["pair", h][:], planes[h][:, 3:4, 0:GROUPS].to_broadcast([P, 2, GROUPS]), ALU.max
             )
+            nc.vector.tensor_tensor(work["low", h][:], work["even", h][:], work["odd", h][:], ALU.min)
 
-        def low(h, v):
-            nc.vector.tensor_tensor(work["low", h][:, :, v], work["even", h][:, :, v], work["odd", h][:, :, v], ALU.min)
-
-        def side(h, v):
-            nc.vector.tensor_tensor(work["side", h][:, :, v], work["shared", h][:, :, v], work["low", h][:, ::-1, v], ALU.max)
-
-        def meet(h, v):
-            nc.vector.tensor_tensor(both[h][:, v], work["side", h][:, 0, v], work["side", h][:, 1, v], ALU.min)
-
-        def last(h, v):
-            nc.vector.tensor_tensor(result[h][:, v], both[h][:, v], planes[h][:, 3, v], ALU.max)
-
-        def store(h):
-            nc.sync.dma_start(out[:, h * GROUPS : (h + 1) * GROUPS], result[h][:])
-
-        grouped = {}
-        for o in range(PASSES):
-            grouped["b", o] = cast("b", o, 1.0)
-            grouped["a", o] = cast("a", o, -1.0)
-
-        gather(0, 1, "picked01")
-        gather(0, 0, "picked00")
-        gather_scales(1, "picked_scales1")
-        quantise("b", 0, grouped["b", 0])
-        quantise("a", 0, grouped["a", 0])
+        gather_first()
+        quantise(0)
+        gather_scales(1, "slot_a0")
         multiply("b", 0, 1)
         multiply("a", 0, 1)
-        gather_scales(0, "slot_a0")
+        quantise(1)
+        gather_scales(0, "slot_b1")
         multiply("b", 0, 0)
         multiply("a", 0, 0)
-        gather(1, 1, "picked11")
-        quantise("b", 1, grouped["b", 1])
-        quantise("a", 1, grouped["a", 1])
+        gather_second(1, "picked11")
         multiply("b", 1, 1)
-        multiply("a", 1, 1)
         evacuate(1)
-        gather(1, 0, "slot_a1")
+        quantise(2)
+        multiply("a", 1, 1)
+        gather_second(0, "slot_a1")
         multiply("b", 1, 0)
         multiply("a", 1, 0)
         evacuate(0)
 
-        whole = slice(0, GROUPS)
-        parts = (slice(0, GROUPS // 2), slice(GROUPS // 2, GROUPS))
-        own(1, "even", 0)
-        own(1, "odd", 1)
-        shared(1)
-        low(1, whole)
-        side(1, whole)
-        own(0, "even", 0)
-        meet(1, whole)
-        own(0, "odd", 1)
-        last(1, whole)
-        store(1)
-        shared(0)
-        for step in (low, side, meet, last):
-            for v in parts:
-                step(0, v)
-        store(0)
+        first_stage(1)
+        first_stage(0)
+        for h in (1, 0):
+            nc.vector.tensor_tensor(work["side", h][:], work["shared", h][:], work["low", h][:, ::-1, :], ALU.max)
+        for h in (1, 0):
+            nc.vector.tensor_tensor(result[h][:], work["side", h][:, 0, :], work["side", h][:, 1, :], ALU.min)
+            nc.sync.dma_start(out[:, h * GROUPS : (h + 1) * GROUPS], result[h][:])

@@ -39,11 +39,17 @@ def tile_picked_ystl_hard_p_kernel(tc, x_words, x_scales, w1, w2, ca, thb, offs,
         raw = {}
 
         def load_scales():
-            for q in range(4):
-                nc.sync.dma_start(
+            for q, queue in ((0, nc.gpsimd), (1, nc.sync)):
+                queue.dma_start(
                     table_scales[32 * q : 32 * q + 8, :].bitcast(I32),
                     x_scales[:, 4 * q : 4 * q + 4, :].bitcast(I32),
                 )
+            for q in (2, 3):
+                for o in range(PASSES):
+                    nc.sync.dma_start(
+                        table_scales[32 * q + 4 * o : 32 * q + 4 * o + 4, :].bitcast(I32),
+                        x_scales[o, 4 * q : 4 * q + 4, :].bitcast(I32),
+                    )
 
         def load_words(o):
             nc.sync.dma_start(table_words[o][:], x_words[o].rearrange("p n t -> p (n t)").bitcast(I32))
@@ -53,8 +59,8 @@ def tile_picked_ystl_hard_p_kernel(tc, x_words, x_scales, w1, w2, ca, thb, offs,
             nc.sync.dma_start(raw[key, o][:], w[o * K_PASS : (o + 1) * K_PASS, :].rearrange("(p j) m -> p j m", j=PACK))
 
         nc.vector.memset(table_scales[:].bitcast(I32), 0)
-        nc.sync.dma_start(offsets[:], offs)
         load_words(0)
+        nc.sync.dma_start(offsets[:], offs)
         load_weight("b", w2, 0)
         load_weight("a", w1, 0)
         load_scales()

@@ -125,11 +125,30 @@ def tile_picked_ystl_hard_p_kernel(tc, x_words, x_scales, w1, w2, ca, thb, offs,
         planes = [t[:].rearrange("p (d s) -> p d s", d=D) for t in b0]
         nc.vector.memset(planes[1][:, 0:3, GROUPS : GROUPS + 1], PAD)
 
+        lifted = [keep.tile([P, 2, PITCH], F32, name=f"lifted{h}", align_bytes=64) for h in range(2)]
+        both_col = keep.tile([P, 1], F32, name="both_col")
+        nc.scalar.activation(both_col[:], thb_col[:], ACT.Identity, bias=ca_col[:])
+        nc.scalar.activation(
+            lifted[1][:, :, GROUPS : GROUPS + 1], ca_col[:].unsqueeze(1).to_broadcast([P, 2, 1]), ACT.Copy, bias=PAD
+        )
+
         def evacuate(h):
+            nc.scalar.activation(
+                lifted[h][:, :, 0:GROUPS],
+                acc["b", h][:].rearrange("p (v e d) -> p d e v", e=2, d=2)[:, 0],
+                ACT.Identity,
+                bias=both_col[:],
+            )
             nc.scalar.activation(
                 planes[h][:, :, 0:GROUPS], acc["b", h][:].rearrange("p (v d) -> p d v", d=D), ACT.Identity, bias=thb_col[:]
             )
             if h == 1:
+                nc.scalar.activation(
+                    lifted[0][:, :, GROUPS : GROUPS + 1],
+                    acc["b", h][:, 0:4].rearrange("p (e d) -> p e d", d=2)[:, :, 0:1],
+                    ACT.Identity,
+                    bias=both_col[:],
+                )
                 nc.scalar.activation(
                     planes[0][:, 0:3, GROUPS : GROUPS + 1],
                     acc["b", h][:, 0:3].rearrange("p (d v) -> p d v", v=1),
@@ -145,6 +164,9 @@ def tile_picked_ystl_hard_p_kernel(tc, x_words, x_scales, w1, w2, ca, thb, offs,
         result = [keep.tile([P, GROUPS], F32, name=f"result{h}", align_bytes=64) for h in range(2)]
 
         def first_stage(h):
+            minus_a = acc["a", h][:].rearrange("p (v e d) -> p d e v", e=2, d=2)
+            for d, name in enumerate(("even", "odd")):
+                nc.vector.tensor_tensor(work[name, h][:], minus_a[:, d], lifted[h][:, :, d : GROUPS + d], ALU.max)
             span = 2 * (PITCH - 1)
             nc.vector.tensor_tensor(
                 work["pair", h][:],
@@ -152,15 +174,10 @@ def tile_picked_ystl_hard_p_kernel(tc, x_words, x_scales, w1, w2, ca, thb, offs,
                 b0[h][:, PITCH + 1 : PITCH + 1 + span].rearrange("p (c s) -> p c s", c=2)[:, :, 0:GROUPS],
                 ALU.max,
             )
-            minus_a = acc["a", h][:].rearrange("p (v e d) -> p d e v", e=2, d=2)
-            for d, name in enumerate(("even", "odd")):
-                nc.vector.scalar_tensor_tensor(
-                    work[name, h][:], minus_a[:, d], ca_col[:], planes[h][:, 0::2, d : GROUPS + d], ALU.subtract, ALU.max
-                )
+            nc.vector.tensor_tensor(work["low", h][:], work["even", h][:], work["odd", h][:], ALU.min)
             nc.vector.tensor_tensor(
                 work["shared", h][:], work["pair", h][:], planes[h][:, 3:4, 0:GROUPS].to_broadcast([P, 2, GROUPS]), ALU.max
             )
-            nc.vector.tensor_tensor(work["low", h][:], work["even", h][:], work["odd", h][:], ALU.min)
 
         gather_first()
         quantise(0)
@@ -184,7 +201,9 @@ def tile_picked_ystl_hard_p_kernel(tc, x_words, x_scales, w1, w2, ca, thb, offs,
         first_stage(1)
         first_stage(0)
         for h in (1, 0):
-            nc.vector.tensor_tensor(work["side", h][:], work["shared", h][:], work["low", h][:, ::-1, :], ALU.max)
+            nc.vector.scalar_tensor_tensor(
+                work["side", h][:], work["low", h][:, ::-1, :], ca_col[:], work["shared", h][:], ALU.subtract, ALU.max
+            )
         for h in (1, 0):
             nc.vector.tensor_tensor(result[h][:], work["side", h][:, 0, :], work["side", h][:, 1, :], ALU.min)
             nc.sync.dma_start(out[:, h * GROUPS : (h + 1) * GROUPS], result[h][:])

from contextlib import ExitStack

import concourse.mybir as mybir

K, T, S, D, N = 1024, 2048, 1024, 4, 128
FLOPS = 2 * K * (2 * N) * S

F32 = mybir.dt.float32
BF16 = mybir.dt.bfloat16
I32 = mybir.dt.int32
U32 = mybir.dt.uint32
U16 = mybir.dt.uint16
U8 = mybir.dt.uint8
FP8X4 = mybir.dt.float8_e4m3fn_x4
ALU = mybir.AluOpType
ACT = mybir.ActivationFunctionType

P = 128
PACK = 4
K_PASS = P * PACK
PASSES = K // K_PASS
HALF = 512
GROUPS = HALF // D
PITCH = GROUPS + 4
PAD = -6.0


def tile_picked_ystl_hard_p_kernel(tc, x_words, x_scales, w1, w2, ca, thb, offs, out):
    nc = tc.nc
    with ExitStack() as ctx:
        keep = ctx.enter_context(tc.tile_pool(name="keep", bufs=1))
        psum = ctx.enter_context(tc.psum_pool(name="psum", bufs=1))

        offsets = keep.tile([P, S // 16], U16, name="offsets")
        table_scales = keep.tile([P, T], U8, name="table_scales", align_bytes=64)
        table_words = [keep.tile([P, T], I32, name=f"table_words{o}", align_bytes=64) for o in range(PASSES)]
        thb_col = keep.tile([P, 1], F32, name="thb_col")
        ca_col = keep.tile([P, 1], F32, name="ca_col")
        raw = {}

        def load_scales():
            for q, queue in ((0, nc.gpsimd), (1, nc.sync)):
                queue.dma_start(
                    table_scales[32 * q : 32 * q + 8, :].bitcast(I32),
                    x_scales[:, 4 * q : 4 * q + 4, :].bitcast(I32),
                )
            for q in (2, 3):
                for o in range(PASSES):
                    nc.sync.dma_start(
                        table_scales[32 * q + 4 * o : 32 * q + 4 * o + 4, :].bitcast(I32),
                        x_scales[o, 4 * q : 4 * q + 4, :].bitcast(I32),
                    )

        def load_words(o):
            nc.sync.dma_start(table_words[o][:], x_words[o].rearrange("p n t -> p (n t)").bitcast(I32))

        def load_weight(key, w, o):
            raw[key, o] = keep.tile([P, PACK, N], F32, name=f"raw_{key}{o}", tag=f"slot_{key}{o}", align_bytes=64)
            nc.sync.dma_start(raw[key, o][:], w[o * K_PASS : (o + 1) * K_PASS, :].rearrange("(p j) m -> p j m", j=PACK))

        nc.vector.memset(table_scales[:].bitcast(I32), 0)
        load_words(0)
        nc.sync.dma_start(offsets[:], offs)
        load_weight("b", w2, 0)
        load_weight("a", w1, 0)
        load_scales()
        load_weight("b", w2, 1)
        load_words(1)
        load_weight("a", w1, 1)
        nc.sync.dma_start(thb_col[:], thb)
        nc.sync.dma_start(ca_col[:], ca)

        order = (("b", 0), ("a", 0), ("b", 1), ("a", 1))
        spans = ((0, 2), (2, 3), (3, 4))
        grouped = [keep.tile([P, hi - lo, N, PACK], BF16, name=f"grouped{lo}", align_bytes=64) for lo, hi in spans]
        codes = [keep.tile([P, (hi - lo) * N], U32, name=f"codes{lo}", align_bytes=64) for lo, hi in spans]
        scales = [keep.tile([P, (hi - lo) * N], U8, name=f"scales{lo}", align_bytes=64) for lo, hi in spans]
        where = {order[i]: (s, i - lo) for s, (lo, hi) in enumerate(spans) for i in range(lo, hi)}

        for key, o in order:
            s, i = where[key, o]
            nc.scalar.activation(
                grouped[s][:, i], raw[key, o][:].rearrange("p j m -> p m j"), ACT.Copy, scale=(1.0 if key == "b" else -1.0)
            )

        def quantise(s):
            nc.vector.quantize_mx(
                out=codes[s][:].bitcast(FP8X4), scales=scales[s][:], in_=grouped[s][:].rearrange("p i m j -> p (i m j)")
            )

        picked, picked_scales = {}, {}

        def gather_scales(h, tag):
            picked_scales[h] = keep.tile([P, HALF], U8, name=f"picked_scales{h}", tag=tag, align_bytes=64)
            cols = slice(h * HALF // 16, (h + 1) * HALF // 16)
            nc.vector.tensor_copy(picked_scales[h][:], table_scales[:].indirect(offsets[:, cols]))

        def gather_first():
            whole = keep.tile([P, S], U32, name="picked0", align_bytes=64)
            nc.vector.tensor_copy(whole[:], table_words[0][:].bitcast(U32).indirect(offsets[:]))
            for h in range(2):
                picked[0, h] = whole[:, h * HALF : (h + 1) * HALF]

        def gather_second(h, tag):
            part = keep.tile([P, HALF], U32, name=f"picked1{h}", tag=tag, align_bytes=64)
            cols = slice(h * HALF // 16, (h + 1) * HALF // 16)
            nc.vector.tensor_copy(part[:], table_words[1][:].bitcast(U32).indirect(offsets[:, cols]))
            picked[1, h] = part[:]

        acc = {(key, h): psum.tile([P, HALF], F32, name=f"acc_{key}{h}") for key in ("a", "b") for h in range(2)}

        def multiply(key, o, h):
            s, i = where[key, o]
            nc.tensor.matmul_mx(
                out=acc[key, h][:],
                lhsT=codes[s][:, i * N : (i + 1) * N].bitcast(FP8X4),
                lhsT_scale=scales[s][:, i * N : (i + 1) * N],
                rhs=picked[o, h].bitcast(FP8X4),
                rhs_scale=picked_scales[h][4 * o : P, :],
                start=(o == 0),
                stop=(o == PASSES - 1),
            )

        b0 = [keep.tile([P, D * PITCH], F32, name=f"b0_{h}", align_bytes=64) for h in range(2)]
        planes = [t[:].rearrange("p (d s) -> p d s", d=D) for t in b0]
        nc.vector.memset(planes[1][:, 0:3, GROUPS : GROUPS + 1], PAD)

        lifted = [keep.tile([P, 2, PITCH], F32, name=f"lifted{h}", align_bytes=64) for h in range(2)]
        both_col = keep.tile([P, 1], F32, name="both_col")
        nc.scalar.activation(both_col[:], thb_col[:], ACT.Identity, bias=ca_col[:])
        nc.scalar.activation(
            lifted[1][:, :, GROUPS : GROUPS + 1], ca_col[:].unsqueeze(1).to_broadcast([P, 2, 1]), ACT.Copy, bias=PAD
        )

        def evacuate(h):
            nc.scalar.activation(
                lifted[h][:, :, 0:GROUPS],
                acc["b", h][:].rearrange("p (v e d) -> p d e v", e=2, d=2)[:, 0],
                ACT.Identity,
                bias=both_col[:],
            )
            nc.scalar.activation(
                planes[h][:, :, 0:GROUPS], acc["b", h][:].rearrange("p (v d) -> p d v", d=D), ACT.Identity, bias=thb_col[:]
            )
            if h == 1:
                nc.scalar.activation(
                    lifted[0][:, :, GROUPS : GROUPS + 1],
                    acc["b", h][:, 0:4].rearrange("p (e d) -> p e d", d=2)[:, :, 0:1],
                    ACT.Identity,
                    bias=both_col[:],
                )
                nc.scalar.activation(
                    planes[0][:, 0:3, GROUPS : GROUPS + 1],
                    acc["b", h][:, 0:3].rearrange("p (d v) -> p d v", v=1),
                    ACT.Identity,
                    bias=thb_col[:],
                )

        work = {
            (name, h): keep.tile([P, 2, GROUPS], F32, name=f"{name}{h}", align_bytes=64)
            for name in ("pair", "shared", "even", "odd", "low", "side")
            for h in range(2)
        }
        result = [keep.tile([P, GROUPS], F32, name=f"result{h}", align_bytes=64) for h in range(2)]

        def first_stage(h):
            minus_a = acc["a", h][:].rearrange("p (v e d) -> p d e v", e=2, d=2)
            for d, name in enumerate(("even", "odd")):
                nc.vector.tensor_tensor(work[name, h][:], minus_a[:, d], lifted[h][:, :, d : GROUPS + d], ALU.max)
            span = 2 * (PITCH - 1)
            nc.vector.tensor_tensor(
                work["pair", h][:],
                b0[h][:, 1 : 1 + span].rearrange("p (c s) -> p c s", c=2)[:, :, 0:GROUPS],
                b0[h][:, PITCH + 1 : PITCH + 1 + span].rearrange("p (c s) -> p c s", c=2)[:, :, 0:GROUPS],
                ALU.max,
            )
            nc.vector.tensor_tensor(work["low", h][:], work["even", h][:], work["odd", h][:], ALU.min)
            nc.vector.tensor_tensor(
                work["shared", h][:], work["pair", h][:], planes[h][:, 3:4, 0:GROUPS].to_broadcast([P, 2, GROUPS]), ALU.max
            )

        gather_first()
        quantise(0)
        gather_scales(1, "slot_a0")
        multiply("b", 0, 1)
        multiply("a", 0, 1)
        quantise(1)
        gather_scales(0, "slot_b1")
        multiply("b", 0, 0)
        multiply("a", 0, 0)
        gather_second(1, "picked11")
        multiply("b", 1, 1)
        evacuate(1)
        quantise(2)
        multiply("a", 1, 1)
        gather_second(0, "slot_a1")
        multiply("b", 1, 0)
        multiply("a", 1, 0)
        evacuate(0)

        first_stage(1)
        first_stage(0)
        for h in (1, 0):
            nc.vector.scalar_tensor_tensor(
                work["side", h][:], work["low", h][:, ::-1, :], ca_col[:], work["shared", h][:], ALU.subtract, ALU.max
            )
        for h in (1, 0):
            nc.vector.tensor_tensor(result[h][:], work["side", h][:, 0, :], work["side", h][:, 1, :], ALU.min)
            nc.sync.dma_start(out[:, h * GROUPS : (h + 1) * GROUPS], result[h][:])
